import numpy as np
import ml_dtypes


def mxq(x, axis, fmt="e4m3"):
    dtype, down = {"e4m3": (ml_dtypes.float8_e4m3fn, 7), "e5m2": (ml_dtypes.float8_e5m2, 14)}[fmt]
    v = np.moveaxis(np.asarray(x, np.float32).astype(ml_dtypes.bfloat16).astype(np.float64), axis, -1)
    blocks = v.reshape(v.shape[:-1] + (-1, 32))
    amax = np.abs(blocks).max(-1, keepdims=True)
    byte = np.maximum(np.where(amax > 0, np.frexp(amax)[1] - 1 + 127, 0) - down, 1)
    scale = np.exp2(byte - 127.0)
    codes = (blocks / scale).astype(np.float32).astype(dtype).astype(np.float64)
    return np.moveaxis((codes * scale).reshape(v.shape), -1, axis)


WIDE = False


def mx_kscale(k):
    if not WIDE:
        return np.ones(k)
    levels = np.array([10, -10, 5, -5, 0])
    if k % 512:
        return np.exp2(np.random.permutation(np.resize(levels, k // 32))).repeat(32)
    a = np.empty((k // 512, 16))
    for p in range(k // 512):
        a[p, :8] = np.random.permutation(np.resize(levels, 8))
        for g in range(8):
            far = levels[np.abs(levels - a[p, g]) >= 10]
            a[p, g + 8] = far[np.random.randint(len(far))]
    return np.exp2(a.ravel()).repeat(32)


def f64(x):
    return np.asarray(x).astype(np.float64)


def striped(idx):
    return np.tile(idx.reshape(-1, 16).T, (8, 1)).astype(np.uint16)


def unstriped(offs):
    return offs[:16].T.reshape(-1).astype(np.int64)


E2M1 = np.array([0.0, 0.5, 1.0, 1.5, 2.0, 3.0, 4.0, 6.0, -0.0, -0.5, -1.0, -1.5, -2.0, -3.0, -4.0, -6.0])


def pack_weight(w, fmt):
    k, n = w.shape
    w = f64(np.asarray(w, np.float32).astype(ml_dtypes.bfloat16)).reshape(k // 32, 32, n)
    amax = np.abs(w).max(1)
    if fmt == "e4m3":
        byte = np.frexp(amax)[1] - 1 + 127 - 7
    else:
        mant, ex = np.frexp(amax / 6.0)
        byte = np.where(mant > 0.5, ex, ex - 1) + 127
    byte = np.clip(np.where(amax > 0, byte, 1), 1, 254)
    scaled = (w * np.exp2(127.0 - byte)[:, None, :]).reshape(k, n).astype(np.float32)
    by_word = np.ascontiguousarray(scaled.reshape(k // 512, 128, 4, n).transpose(0, 1, 3, 2))
    if fmt == "e4m3":
        words = by_word.astype(ml_dtypes.float8_e4m3fn).view(np.uint8)
    else:
        c = by_word.astype(ml_dtypes.float4_e2m1fn).view(np.uint8) & 0xF
        words = (c[..., 0::2] | (c[..., 1::2] << 4)).reshape(k // 512, 128, 2 * n)
    return np.ascontiguousarray(words), np.ascontiguousarray(byte.astype(np.uint8).reshape(k // 512, 16, n))


def unpack_weight(words, scales, fmt):
    g, _, n = scales.shape
    words = np.ascontiguousarray(words).reshape(g, 128, n, -1)
    if fmt == "e4m3":
        vals = words.view(ml_dtypes.float8_e4m3fn).astype(np.float64)
    else:
        nib = np.empty((g, 128, n, 4), np.uint8)
        nib[..., 0::2] = words & 0xF
        nib[..., 1::2] = words >> 4
        vals = E2M1[nib]
    vals = vals * np.repeat(np.exp2(scales.astype(np.float64) - 127.0), 8, axis=1)[..., None]
    return vals.transpose(0, 1, 3, 2).reshape(g * 512, n)


def gelu(v):
    return 0.5 * v * (1.0 + np.tanh(np.sqrt(2.0 / np.pi) * (v + 0.044715 * v**3)))


def bf(x):
    return np.asarray(x, np.float32).astype(ml_dtypes.bfloat16)


def planes(Y):
    n, m = Y.shape
    b = f64(bf(Y)).reshape(n // 32, 32, m)
    amax = np.abs(b).max(1)
    byte = np.clip(np.where(amax > 0, np.frexp(amax)[1] - 1 + 127 - 7, 1), 1, 254)
    codes = (b * np.exp2(127.0 - byte)[:, None, :]).reshape(n, m).astype(np.float32).astype(ml_dtypes.float8_e4m3fn).view(np.uint8)
    words = codes.reshape(n // 512, 128, 4, m).transpose(0, 1, 3, 2)
    return np.ascontiguousarray(words), np.ascontiguousarray(byte.astype(np.uint8).reshape(n // 512, 16, m))


K, H, N, T, S, T2 = 1024, 1024, 512, 4096, 1024, 2048


def setup_inputs():
    n = np.random.standard_normal
    s = mx_kscale(K)[:, None]
    u = mx_kscale(H)[:, None]
    tab_words, tab_scales = pack_weight(n((K, T)) * s, "e4m3")
    w2_words, w2_scales = pack_weight(1.5 * n((H, N)) / np.sqrt(H) / u, "e2m1")
    return {
        "tab_words": tab_words, "tab_scales": tab_scales,
        "offs": striped(np.random.permutation(T)[:S]),
        "offs2": striped(np.random.permutation(T2)[:S]),
        "w1": (n((K, H)) / np.sqrt(K) / s * u.T).astype(np.float32),
        "wgs": np.exp(0.3 * n((128, S))).astype(np.float32),
        "page0": (n((H, T2)) * u).astype(np.float32),
        "w2_words": w2_words, "w2_scales": w2_scales,
        "slotf": (0.5 * n((N, T2))).astype(np.float32),
    }


def reference(tab_words, tab_scales, offs, offs2, w1, wgs, page0, w2_words, w2_scales, slotf):
    v = unpack_weight(tab_words, tab_scales, "e4m3")[:, unstriped(offs)]
    h = mxq(f64(w1), 0, "e4m3").T @ v
    page = f64(page0).copy()
    page[:, unstriped(offs2)] = np.tile(f64(wgs), (H // 128, 1)) * h
    words, scales = planes(page)
    w2 = unpack_weight(w2_words, w2_scales, "e2m1")
    z = w2.T @ mxq(page, 0, "e4m3")
    y = z / (1.0 + np.exp(-z)) + f64(slotf)
    return y, page, words, scales

@@ -1,0 +1,363 @@
+from contextlib import ExitStack
+
+import concourse.mybir as mybir
+from concourse.masks import make_identity
+
+K, H, N, T, S, T2 = 1024, 1024, 512, 4096, 1024, 2048
+FLOPS = 2 * K * H * S + 2 * H * N * T2
+
+F32 = mybir.dt.float32
+BF16 = mybir.dt.bfloat16
+I32 = mybir.dt.int32
+U32 = mybir.dt.uint32
+U16 = mybir.dt.uint16
+U8 = mybir.dt.uint8
+FP8X4 = mybir.dt.float8_e4m3fn_x4
+FP4X4 = mybir.dt.float4_e2m1fn_x4
+MULT = mybir.AluOpType.mult
+ADD = mybir.AluOpType.add
+SILU = mybir.ActivationFunctionType.Silu
+
+P = 128
+PACK = 4
+PASS = P * PACK
+BANK = 512
+KIB = 1024
+QUADS = 4
+SLICES = H // P
+CHUNKS = T2 // BANK
+RING = 4
+ALIGN = 256
+
+RAW_FIRST = 0
+RAW_SECOND = 16 * KIB
+TABLE = 32 * KIB
+H_RING = 64 * KIB
+Q_RING = 80 * KIB
+SCALES = 96 * KIB
+SECOND_HIDDEN = 100 * KIB
+
+
+def tile_list_clause_prefix_cache_kernel(
+    tc, tab_words, tab_scales, offs, offs2, w1, wgs, page0, w2_words, w2_scales, slotf, out_0, out_1, out_2, out_3
+):
+    nc = tc.nc
+    with ExitStack() as ctx:
+        lists = ctx.enter_context(tc.tile_pool(name="lists", bufs=1))
+        keep = ctx.enter_context(tc.tile_pool(name="keep", bufs=1))
+        shared = ctx.enter_context(tc.tile_pool(name="shared", bufs=1))
+        psum = ctx.enter_context(tc.psum_pool(name="psum", bufs=1))
+
+        def kept(shape, dtype, name):
+            return keep.tile(shape, dtype, name=name, align_bytes=ALIGN)
+
+        def placed(shape, dtype, name, offset):
+            return shared.tile(shape, dtype, name=name, offset=offset, align_bytes=ALIGN)
+
+        def bank(number, name):
+            return psum.tile([P, BANK], F32, name=name, tag="bank%d" % number)
+
+        def page_rows(dram, s):
+            g, t = divmod(s, PACK)
+            return dram[g * PASS : (g + 1) * PASS, :].rearrange("(p t) m -> t p m", t=PACK)[t]
+
+        def w1_rows(a, g):
+            return w1[a * PASS : (a + 1) * PASS, g * PASS : (g + 1) * PASS].rearrange("(p j) c -> p j c", j=PACK)
+
+        picks = lists.tile([P, S // 16], U16, name="picks")
+        slots = lists.tile([P, S // 16], U16, name="slots")
+
+        table_scales = placed([P, T], U8, "table_scales", SCALES)
+        w2_planes = kept([P, 2, N], U8, "w2_planes")
+        nc.vector.memset(table_scales[:].bitcast(I32), 0)
+        nc.vector.memset(w2_planes[:].rearrange("p a c -> p (a c)").bitcast(I32), 0)
+        identity = kept([P, P], F32, "identity")
+        make_identity(nc, identity[:])
+        for q in range(QUADS):
+            nc.gpsimd.dma_start(
+                out=table_scales[32 * q : 32 * q + 8, :].bitcast(I32),
+                in_=tab_scales[:, 4 * q : 4 * q + 4, :].bitcast(I32),
+            )
+        for q in range(QUADS):
+            nc.gpsimd.dma_start(
+                out=w2_planes[32 * q : 32 * q + 4, :, :].bitcast(I32),
+                in_=w2_scales[:, 4 * q : 4 * q + 4, :].rearrange("a r c -> r a c").bitcast(I32),
+            )
+
+        wgs_rows = placed([P, S], F32, "wgs_rows", Q_RING + 3 * 4 * KIB)
+        nc.sync.dma_start(out=wgs_rows[:], in_=wgs)
+        raw_first = [placed([P, PACK, PASS], F32, "raw_first%d" % a, RAW_FIRST + a * 8 * KIB) for a in range(2)]
+        for a in range(2):
+            nc.sync.dma_start(out=raw_first[a][:], in_=w1_rows(a, 0))
+        nc.sync.dma_start(picks[:], offs)
+        table = [placed([P, T], U32, "table%d" % a, TABLE + a * 16 * KIB) for a in range(2)]
+        for a in range(2):
+            nc.sync.dma_start(
+                out=table[a][:].bitcast(I32), in_=tab_words[a].rearrange("p n t -> p (n t)").bitcast(I32)
+            )
+        nc.sync.dma_start(slots[:], offs2)
+        pages = [kept([P, T2], F32, "page%d" % s) for s in range(SLICES)]
+
+        def load_page(s):
+            nc.sync.dma_start(out=pages[s][:], in_=page_rows(page0, s))
+
+        load_page(0)
+        load_page(1)
+        raw_second = placed([P, 2, PACK, PASS], F32, "raw_second", RAW_SECOND)
+        for a in range(2):
+            nc.sync.dma_start(out=raw_second[:, a, :, :], in_=w1_rows(a, 1))
+        w2_codes = kept([P, 2, 2 * N], U8, "w2_codes")
+        nc.sync.dma_start(out=w2_codes[:].bitcast(I32), in_=w2_words.rearrange("a p c -> p a c").bitcast(I32))
+
+        turned = [bank(6 + b, "turned%d" % b) for b in range(2)]
+        for j in range(S // P):
+            nc.tensor.transpose(
+                turned[j // 4][:, (j % 4) * P : (j % 4 + 1) * P], wgs_rows[:, j * P : (j + 1) * P], identity[:]
+            )
+        factors = [kept([P, S], F32, "factor%d" % t) for t in range(PACK)]
+        back = {}
+
+        def repeat_and_turn_back(t):
+            repeated = placed([P, S], F32, "repeated%d" % t, H_RING + t * 4 * KIB)
+            for b in range(2):
+                picked = turned[b][:].rearrange("p (j q t) -> p j t q", j=4, t=PACK)[:, :, t : t + 1, :]
+                nc.scalar.copy(
+                    out=repeated[:, b * BANK : (b + 1) * BANK].rearrange("p (j r q) -> p j r q", j=4, r=QUADS),
+                    in_=picked.to_broadcast([P, 4, QUADS, 32]),
+                )
+            for b in range(2):
+                back[t, b] = bank(2 * (t % 3) + b, "back%d_%d" % (t, b))
+                for j in range(4):
+                    col = b * BANK + j * P
+                    nc.tensor.transpose(back[t, b][:, j * P : (j + 1) * P], repeated[:, col : col + P], identity[:])
+
+        def keep_factor(t):
+            for b in range(2):
+                nc.scalar.copy(out=factors[t][:, b * BANK : (b + 1) * BANK], in_=back[t, b][:])
+
+        for t in range(PACK):
+            repeat_and_turn_back(t)
+            if t > 0:
+                keep_factor(t - 1)
+        keep_factor(PACK - 1)
+
+        w1_codes = {}
+        w1_planes = {}
+        w1_grouped = {}
+
+        def group_w1(a, g, raw, grouped, copy):
+            copy(
+                out=grouped.rearrange("p (t m j) -> p m j t", t=PACK, j=PACK),
+                in_=raw.rearrange("p j (m t) -> p m j t", t=PACK),
+            )
+            w1_grouped[a, g] = grouped
+
+        def quantize_w1(a, g):
+            if g == 0:
+                w1_codes[a, g] = kept([P, PASS], U32, "w1_codes%d_%d" % (a, g))
+            else:
+                w1_codes[a, g] = placed([P, PASS], U32, "w1_codes%d_%d" % (a, g), SECOND_HIDDEN + a * 2 * KIB)
+            w1_planes[a, g] = kept([P, PASS], U8, "w1_planes%d_%d" % (a, g))
+            nc.vector.quantize_mx(
+                out=w1_codes[a, g][:].bitcast(FP8X4), scales=w1_planes[a, g][:], in_=w1_grouped[a, g]
+            )
+
+        for a in range(2):
+            grouped = placed([P, PACK * PASS], BF16, "w1_grouped%d" % a, Q_RING + a * 4 * KIB)
+            group_w1(a, 0, raw_first[a][:], grouped[:], nc.vector.tensor_copy)
+        for a in range(2):
+            quantize_w1(a, 0)
+
+        features = {}
+
+        def load_features(n):
+            offset = RAW_FIRST + n * 8 * KIB if n < 2 else TABLE + n * 8 * KIB
+            features[n] = placed([P, T2], F32, "features%d" % n, offset)
+            nc.sync.dma_start(out=features[n][:], in_=slotf[n * P : (n + 1) * P, :])
+
+        load_features(0)
+        for s in range(2, 6):
+            load_page(s)
+
+        picked_scales = kept([P, S], U8, "picked_scales")
+        nc.vector.tensor_copy(picked_scales[:], table_scales[:].indirect(picks[:]))
+        picked_words = [placed([P, S], U32, "picked_words%d" % a, (SCALES, TABLE)[a]) for a in range(2)]
+        nc.vector.tensor_copy(picked_words[0][:], table[0][:].indirect(picks[:]))
+        for b in range(2):
+            nc.vector.tensor_copy(
+                picked_words[1][:, b * BANK : (b + 1) * BANK], table[1][:].indirect(picks[:, 32 * b : 32 * (b + 1)])
+            )
+
+        hidden = {}
+
+        def make_hidden(s):
+            g, t = divmod(s, PACK)
+            rows = slice(t * P, (t + 1) * P)
+            slot = (0, 0, 2, 3, 1, 0, 2, 3)[s]
+            hidden[s] = placed([P, S], F32, "hidden%d" % s, SECOND_HIDDEN if s == 1 else H_RING + slot * 4 * KIB)
+            for b in range(2):
+                cols = slice(b * BANK, (b + 1) * BANK)
+                acc = bank(2 * (s % 2) + b, "h%d_%d" % (s, b))
+                for a in range(2):
+                    nc.tensor.matmul_mx(
+                        out=acc[:],
+                        lhsT=w1_codes[a, g][:, rows].bitcast(FP8X4),
+                        lhsT_scale=w1_planes[a, g][:, rows],
+                        rhs=picked_words[a][:, cols].bitcast(FP8X4),
+                        rhs_scale=picked_scales[4 * a : P, cols],
+                        start=(a == 0),
+                        stop=(a == 1),
+                    )
+                nc.scalar.copy(out=hidden[s][:, cols], in_=acc[:])
+
+        def scatter(s, pieces):
+            width = S // pieces
+            for b in range(pieces):
+                cols = slice(b * width, (b + 1) * width)
+                nc.vector.tensor_tensor(
+                    pages[s][:].indirect(slots[:, b * width // 16 : (b + 1) * width // 16]),
+                    hidden[s][:, cols],
+                    factors[s % PACK][:, cols],
+                    MULT,
+                )
+
+        def store_page(s):
+            nc.sync.dma_start(out=page_rows(out_1, s), in_=pages[s][:])
+
+        pairs = {}
+
+        def round_chunk(s, c):
+            g, t = divmod(s, PACK)
+            if t == 0:
+                pairs[g, c] = placed([P, PACK * BANK], BF16, "pairs%d_%d" % (g, c), RAW_SECOND + c * 4 * KIB)
+            halves = pairs[g, c][:].rearrange("p (u m e) -> p u m e", u=2, e=2)
+            nc.scalar.copy(out=halves[:, t // 2, :, t % 2], in_=pages[s][:, c * BANK : (c + 1) * BANK])
+
+        def round_page(s):
+            for c in range(CHUNKS):
+                round_chunk(s, c)
+
+        woven = {}
+
+        def weave(g, c, copy):
+            woven[g, c] = placed([P, PACK * BANK], BF16, "woven%d_%d" % (g, c), Q_RING + c * 4 * KIB)
+            copy(
+                out=woven[g, c][:].bitcast(F32).rearrange("p (m u) -> p m u", u=2),
+                in_=pairs[g, c][:].bitcast(F32).rearrange("p (u m) -> p m u", u=2),
+            )
+
+        page_codes = [kept([P, T2], U32, "page_codes%d" % g) for g in range(2)]
+        page_planes = [kept([P, T2], U8, "page_planes%d" % g) for g in range(2)]
+
+        def quantize_chunk(g, c):
+            cols = slice(c * BANK, (c + 1) * BANK)
+            nc.vector.quantize_mx(
+                out=page_codes[g][:, cols].bitcast(FP8X4), scales=page_planes[g][:, cols], in_=woven[g, c][:]
+            )
+
+        def store_codes(g, cols):
+            words = out_2[g].rearrange("p m t -> p (m t)").bitcast(I32)
+            nc.sync.dma_start(out=words[:, cols], in_=page_codes[g][:, cols].bitcast(I32))
+
+        def store_planes(g):
+            for q in range(QUADS):
+                nc.sync.dma_start(
+                    out=out_3[g, 4 * q : 4 * q + 4, :].bitcast(I32),
+                    in_=page_planes[g][32 * q : 32 * q + 4, :].bitcast(I32),
+                )
+
+        sums = {}
+
+        def layer_pass(n, c, g):
+            if g == 0:
+                sums[n, c] = bank(2 * n + c % 2, "z%d_%d" % (n, c))
+            cols = slice(c * BANK, (c + 1) * BANK)
+            nc.tensor.matmul_mx(
+                out=sums[n, c][:],
+                lhsT=w2_codes[:, g, 2 * n * P : 2 * (n + 1) * P].bitcast(FP4X4),
+                lhsT_scale=w2_planes[:, g, n * P : (n + 1) * P],
+                rhs=page_codes[g][:, cols].bitcast(FP8X4),
+                rhs_scale=page_planes[g][:, cols],
+                start=(g == 0),
+                stop=(g == 1),
+            )
+
+        for s in range(PACK):
+            make_hidden(s)
+        scatter(0, 2)
+        second_grouped = placed([P, 2 * PACK * PASS], BF16, "second_grouped", H_RING)
+        for a in range(2):
+            part = second_grouped[:, a * PACK * PASS : (a + 1) * PACK * PASS]
+            group_w1(a, 1, raw_second[:, a, :, :], part, nc.scalar.copy)
+        store_page(0)
+        load_features(1)
+        round_page(0)
+        scatter(1, 1)
+        store_page(1)
+        load_page(6)
+        round_page(1)
+        for a in range(2):
+            quantize_w1(a, 1)
+        scatter(2, 1)
+        store_page(2)
+        load_features(2)
+        make_hidden(4)
+        round_page(2)
+        make_hidden(5)
+        scatter(3, 1)
+        store_page(3)
+        load_page(7)
+        load_features(3)
+        round_page(3)
+        make_hidden(6)
+        scatter(4, 1)
+        store_page(4)
+        for c in range(CHUNKS):
+            weave(0, c, nc.scalar.copy)
+        make_hidden(7)
+        round_page(4)
+        scatter(5, 1)
+        store_page(5)
+        for c in range(CHUNKS):
+            quantize_chunk(0, c)
+        store_codes(0, slice(0, T2))
+        store_planes(0)
+        round_page(5)
+        for n in range(N // P):
+            for c in range(2):
+                layer_pass(n, c, 0)
+        scatter(6, 1)
+        store_page(6)
+        round_page(6)
+        scatter(7, 1)
+        store_page(7)
+
+        round_page(7)
+        weave(1, 0, nc.vector.tensor_copy)
+        weave(1, 1, nc.vector.tensor_copy)
+        quantize_chunk(1, 0)
+        weave(1, 2, nc.vector.tensor_copy)
+        quantize_chunk(1, 1)
+        store_codes(1, slice(0, T2 // 2))
+        weave(1, 3, nc.scalar.copy)
+        quantize_chunk(1, 2)
+        quantize_chunk(1, 3)
+        store_codes(1, slice(T2 // 2, T2))
+        store_planes(1)
+        for half in range(2):
+            for n in range(N // P):
+                activated = placed([P, 2 * BANK], F32, "activated%d_%d" % (half, n), H_RING + n * 4 * KIB)
+                for b in range(2):
+                    c = 2 * half + b
+                    if half == 1:
+                        layer_pass(n, c, 0)
+                    layer_pass(n, c, 1)
+                    nc.scalar.activation(activated[:, b * BANK : (b + 1) * BANK], sums[n, c][:], SILU)
+                    cols = slice(c * BANK, (c + 1) * BANK)
+                    nc.vector.tensor_tensor(
+                        features[n][:, cols], activated[:, b * BANK : (b + 1) * BANK], features[n][:, cols], ADD
+                    )
+                    last = half == 1 and n == N // P - 1
+                    if last or b == 1:
+                        cols = cols if last else slice(half * 2 * BANK, (half + 1) * 2 * BANK)
+                        nc.sync.dma_start(out=out_0[n * P : (n + 1) * P, cols], in_=features[n][:, cols])

@@ -73,28 +73,29 @@ def tile_list_clause_prefix_cache_kernel(
         nc.vector.memset(w2_planes[:].rearrange("p a c -> p (a c)").bitcast(I32), 0)
         identity = kept([P, P], F32, "identity")
         make_identity(nc, identity[:])
-        for q in range(QUADS):
-            nc.gpsimd.dma_start(
-                out=table_scales[32 * q : 32 * q + 8, :].bitcast(I32),
-                in_=tab_scales[:, 4 * q : 4 * q + 4, :].bitcast(I32),
-            )
-        for q in range(QUADS):
-            nc.gpsimd.dma_start(
-                out=w2_planes[32 * q : 32 * q + 4, :, :].bitcast(I32),
-                in_=w2_scales[:, 4 * q : 4 * q + 4, :].rearrange("a r c -> r a c").bitcast(I32),
-            )
+
+        warm = kept([P, 1], F32, "warm")
+        nc.scalar.activation(warm[:], identity[:, 0:1], SILU)
 
         wgs_rows = placed([P, S], F32, "wgs_rows", Q_RING + 3 * 4 * KIB)
-        nc.sync.dma_start(out=wgs_rows[:], in_=wgs)
+        for b in range(2):
+            nc.sync.dma_start(out=wgs_rows[:, b * BANK : (b + 1) * BANK], in_=wgs[:, b * BANK : (b + 1) * BANK])
         raw_first = [placed([P, PACK, PASS], F32, "raw_first%d" % a, RAW_FIRST + a * 8 * KIB) for a in range(2)]
         for a in range(2):
-            nc.sync.dma_start(out=raw_first[a][:], in_=w1_rows(a, 0))
-        nc.sync.dma_start(picks[:], offs)
+            for j in range(0, PACK, 2):
+                nc.sync.dma_start(out=raw_first[a][:, j : j + 2, :], in_=w1_rows(a, 0)[:, j : j + 2, :])
         table = [placed([P, T], U32, "table%d" % a, TABLE + a * 16 * KIB) for a in range(2)]
+        nc.sync.dma_start(picks[:], offs)
+        words = [tab_words[a].rearrange("p n t -> p (n t)").bitcast(I32) for a in range(2)]
         for a in range(2):
-            nc.sync.dma_start(
-                out=table[a][:].bitcast(I32), in_=tab_words[a].rearrange("p n t -> p (n t)").bitcast(I32)
-            )
+            cols = slice(a * T // 2, (a + 1) * T // 2)
+            nc.sync.dma_start(out=table[0][:, cols].bitcast(I32), in_=words[0][:, cols])
+            for q in range(QUADS):
+                nc.sync.dma_start(
+                    out=table_scales[32 * q + 4 * a : 32 * q + 4 * a + 4, :].bitcast(I32),
+                    in_=tab_scales[a, 4 * q : 4 * q + 4, :].bitcast(I32),
+                )
+        nc.sync.dma_start(out=table[1][:].bitcast(I32), in_=words[1])
         nc.sync.dma_start(slots[:], offs2)
         pages = [kept([P, T2], F32, "page%d" % s) for s in range(SLICES)]
 
@@ -108,6 +109,11 @@ def tile_list_clause_prefix_cache_kernel(
             nc.sync.dma_start(out=raw_second[:, a, :, :], in_=w1_rows(a, 1))
         w2_codes = kept([P, 2, 2 * N], U8, "w2_codes")
         nc.sync.dma_start(out=w2_codes[:].bitcast(I32), in_=w2_words.rearrange("a p c -> p a c").bitcast(I32))
+        for q in range(QUADS):
+            nc.sync.dma_start(
+                out=w2_planes[32 * q : 32 * q + 4, :, :].bitcast(I32),
+                in_=w2_scales[:, 4 * q : 4 * q + 4, :].rearrange("a r c -> r a c").bitcast(I32),
+            )
 
         turned = [bank(6 + b, "turned%d" % b) for b in range(2)]
         for j in range(S // P):
@@ -179,14 +185,16 @@ def tile_list_clause_prefix_cache_kernel(
         for s in range(2, 6):
             load_page(s)
 
-        picked_scales = kept([P, S], U8, "picked_scales")
+        first_words = kept([P, S], U32, "first_words")
+        nc.vector.tensor_copy(first_words[:], table[0][:].indirect(picks[:]))
+        picked_scales = placed([P, S], U8, "picked_scales", TABLE)
         nc.vector.tensor_copy(picked_scales[:], table_scales[:].indirect(picks[:]))
-        picked_words = [placed([P, S], U32, "picked_words%d" % a, (SCALES, TABLE)[a]) for a in range(2)]
-        nc.vector.tensor_copy(picked_words[0][:], table[0][:].indirect(picks[:]))
+        picked_words = {}
         for b in range(2):
-            nc.vector.tensor_copy(
-                picked_words[1][:, b * BANK : (b + 1) * BANK], table[1][:].indirect(picks[:, 32 * b : 32 * (b + 1)])
-            )
+            picked_words[0, b] = first_words[:, b * BANK : (b + 1) * BANK]
+            second_words = placed([P, BANK], U32, "second_words%d" % b, SCALES + b * 2 * KIB)
+            nc.vector.tensor_copy(second_words[:], table[1][:].indirect(picks[:, 32 * b : 32 * (b + 1)]))
+            picked_words[1, b] = second_words[:]
 
         hidden = {}
 
@@ -197,13 +205,13 @@ def tile_list_clause_prefix_cache_kernel(
             hidden[s] = placed([P, S], F32, "hidden%d" % s, SECOND_HIDDEN if s == 1 else H_RING + slot * 4 * KIB)
             for b in range(2):
                 cols = slice(b * BANK, (b + 1) * BANK)
-                acc = bank(2 * (s % 2) + b, "h%d_%d" % (s, b))
+                acc = bank(b, "h%d_%d" % (s, b))
                 for a in range(2):
                     nc.tensor.matmul_mx(
                         out=acc[:],
                         lhsT=w1_codes[a, g][:, rows].bitcast(FP8X4),
                         lhsT_scale=w1_planes[a, g][:, rows],
-                        rhs=picked_words[a][:, cols].bitcast(FP8X4),
+                        rhs=picked_words[a, b].bitcast(FP8X4),
                         rhs_scale=picked_scales[4 * a : P, cols],
                         start=(a == 0),
                         stop=(a == 1),

@@ -36,6 +36,7 @@ H_RING = 64 * KIB
 Q_RING = 80 * KIB
 SCALES = 96 * KIB
 SECOND_HIDDEN = 100 * KIB
+SIXTH_HIDDEN = 104 * KIB
 
 
 def tile_list_clause_prefix_cache_kernel(
@@ -77,15 +78,15 @@ def tile_list_clause_prefix_cache_kernel(
         warm = kept([P, 1], F32, "warm")
         nc.scalar.activation(warm[:], identity[:, 0:1], SILU)
 
-        wgs_rows = placed([P, S], F32, "wgs_rows", Q_RING + 3 * 4 * KIB)
-        for b in range(2):
-            nc.sync.dma_start(out=wgs_rows[:, b * BANK : (b + 1) * BANK], in_=wgs[:, b * BANK : (b + 1) * BANK])
+        wgs_rows = [placed([P, BANK], F32, "wgs_rows%d" % b, Q_RING + (12 + 2 * b) * KIB) for b in range(2)]
+        nc.sync.dma_start(out=wgs_rows[0][:], in_=wgs[:, 0:BANK])
         raw_first = [placed([P, PACK, PASS], F32, "raw_first%d" % a, RAW_FIRST + a * 8 * KIB) for a in range(2)]
         for a in range(2):
             for j in range(0, PACK, 2):
                 nc.sync.dma_start(out=raw_first[a][:, j : j + 2, :], in_=w1_rows(a, 0)[:, j : j + 2, :])
         table = [placed([P, T], U32, "table%d" % a, TABLE + a * 16 * KIB) for a in range(2)]
         nc.sync.dma_start(picks[:], offs)
+        nc.sync.dma_start(slots[:], offs2)
         words = [tab_words[a].rearrange("p n t -> p (n t)").bitcast(I32) for a in range(2)]
         for a in range(2):
             cols = slice(a * T // 2, (a + 1) * T // 2)
@@ -96,7 +97,7 @@ def tile_list_clause_prefix_cache_kernel(
                     in_=tab_scales[a, 4 * q : 4 * q + 4, :].bitcast(I32),
                 )
         nc.sync.dma_start(out=table[1][:].bitcast(I32), in_=words[1])
-        nc.sync.dma_start(slots[:], offs2)
+        nc.sync.dma_start(out=wgs_rows[1][:], in_=wgs[:, BANK:S])
         pages = [kept([P, T2], F32, "page%d" % s) for s in range(SLICES)]
 
         def load_page(s):
@@ -115,37 +116,35 @@ def tile_list_clause_prefix_cache_kernel(
                 in_=w2_scales[:, 4 * q : 4 * q + 4, :].rearrange("a r c -> r a c").bitcast(I32),
             )
 
-        turned = [bank(6 + b, "turned%d" % b) for b in range(2)]
-        for j in range(S // P):
-            nc.tensor.transpose(
-                turned[j // 4][:, (j % 4) * P : (j % 4 + 1) * P], wgs_rows[:, j * P : (j + 1) * P], identity[:]
-            )
-        factors = [kept([P, S], F32, "factor%d" % t) for t in range(PACK)]
+        factor_rows = [kept([P, S], F32, "factor%d" % t) for t in range(PACK)]
+        turned = {}
         back = {}
 
-        def repeat_and_turn_back(t):
-            repeated = placed([P, S], F32, "repeated%d" % t, H_RING + t * 4 * KIB)
-            for b in range(2):
-                picked = turned[b][:].rearrange("p (j q t) -> p j t q", j=4, t=PACK)[:, :, t : t + 1, :]
-                nc.scalar.copy(
-                    out=repeated[:, b * BANK : (b + 1) * BANK].rearrange("p (j r q) -> p j r q", j=4, r=QUADS),
-                    in_=picked.to_broadcast([P, 4, QUADS, 32]),
-                )
-            for b in range(2):
-                back[t, b] = bank(2 * (t % 3) + b, "back%d_%d" % (t, b))
-                for j in range(4):
-                    col = b * BANK + j * P
-                    nc.tensor.transpose(back[t, b][:, j * P : (j + 1) * P], repeated[:, col : col + P], identity[:])
+        def turn_wgs(b):
+            turned[b] = bank(6 + b, "turned%d" % b)
+            for j in range(4):
+                nc.tensor.transpose(turned[b][:, j * P : (j + 1) * P], wgs_rows[b][:, j * P : (j + 1) * P], identity[:])
 
-        def keep_factor(t):
-            for b in range(2):
-                nc.scalar.copy(out=factors[t][:, b * BANK : (b + 1) * BANK], in_=back[t, b][:])
+        def repeat_and_turn_back(t, b):
+            repeated = placed([P, BANK], F32, "repeated%d_%d" % (t, b), Q_RING + (8 + 2 * (t % 2)) * KIB)
+            picked = turned[b][:].rearrange("p (j q t) -> p j t q", j=4, t=PACK)[:, :, t : t + 1, :]
+            nc.scalar.copy(
+                out=repeated[:].rearrange("p (j r q) -> p j r q", j=4, r=QUADS),
+                in_=picked.to_broadcast([P, 4, QUADS, 32]),
+            )
+            back[t, b] = bank(2 + t, "back%d_%d" % (t, b))
+            for j in range(4):
+                nc.tensor.transpose(back[t, b][:, j * P : (j + 1) * P], repeated[:, j * P : (j + 1) * P], identity[:])
 
+        def keep_factor(t, b):
+            nc.scalar.copy(out=factor_rows[t][:, b * BANK : (b + 1) * BANK], in_=back[t, b][:])
+
+        turn_wgs(0)
         for t in range(PACK):
-            repeat_and_turn_back(t)
+            repeat_and_turn_back(t, 0)
             if t > 0:
-                keep_factor(t - 1)
-        keep_factor(PACK - 1)
+                keep_factor(t - 1, 0)
+        keep_factor(PACK - 1, 0)
 
         w1_codes = {}
         w1_planes = {}
@@ -197,53 +196,70 @@ def tile_list_clause_prefix_cache_kernel(
             picked_words[1, b] = second_words[:]
 
         hidden = {}
+        hidden_at = {
+            1: SECOND_HIDDEN,
+            2: H_RING + 8 * KIB,
+            3: H_RING + 12 * KIB,
+            4: H_RING + 4 * KIB,
+            5: SIXTH_HIDDEN,
+            6: RAW_SECOND + 12 * KIB,
+            7: H_RING + 12 * KIB,
+        }
 
-        def make_hidden(s):
+        def hidden_half(s, b, target):
             g, t = divmod(s, PACK)
             rows = slice(t * P, (t + 1) * P)
-            slot = (0, 0, 2, 3, 1, 0, 2, 3)[s]
-            hidden[s] = placed([P, S], F32, "hidden%d" % s, SECOND_HIDDEN if s == 1 else H_RING + slot * 4 * KIB)
-            for b in range(2):
-                cols = slice(b * BANK, (b + 1) * BANK)
-                acc = bank(b, "h%d_%d" % (s, b))
-                for a in range(2):
-                    nc.tensor.matmul_mx(
-                        out=acc[:],
-                        lhsT=w1_codes[a, g][:, rows].bitcast(FP8X4),
-                        lhsT_scale=w1_planes[a, g][:, rows],
-                        rhs=picked_words[a, b].bitcast(FP8X4),
-                        rhs_scale=picked_scales[4 * a : P, cols],
-                        start=(a == 0),
-                        stop=(a == 1),
-                    )
-                nc.scalar.copy(out=hidden[s][:, cols], in_=acc[:])
-
-        def scatter(s, pieces):
-            width = S // pieces
-            for b in range(pieces):
-                cols = slice(b * width, (b + 1) * width)
-                nc.vector.tensor_tensor(
-                    pages[s][:].indirect(slots[:, b * width // 16 : (b + 1) * width // 16]),
-                    hidden[s][:, cols],
-                    factors[s % PACK][:, cols],
-                    MULT,
+            acc = bank(b, "h%d_%d" % (s, b))
+            for a in range(2):
+                nc.tensor.matmul_mx(
+                    out=acc[:],
+                    lhsT=w1_codes[a, g][:, rows].bitcast(FP8X4),
+                    lhsT_scale=w1_planes[a, g][:, rows],
+                    rhs=picked_words[a, b].bitcast(FP8X4),
+                    rhs_scale=picked_scales[4 * a : P, b * BANK : (b + 1) * BANK],
+                    start=(a == 0),
+                    stop=(a == 1),
                 )
+            nc.scalar.copy(out=target, in_=acc[:])
+
+        def make_hidden(s):
+            hidden[s] = placed([P, S], F32, "hidden%d" % s, hidden_at[s])
+            for b in range(2):
+                hidden_half(s, b, hidden[s][:, b * BANK : (b + 1) * BANK])
+
+        def scatter_part(s, values, first, width):
+            nc.vector.tensor_tensor(
+                pages[s][:].indirect(slots[:, first // 16 : (first + width) // 16]),
+                values,
+                factor_rows[s % PACK][:, first : first + width],
+                MULT,
+            )
+
+        def scatter(s):
+            scatter_part(s, hidden[s][:], 0, S)
 
         def store_page(s):
             nc.sync.dma_start(out=page_rows(out_1, s), in_=pages[s][:])
 
         pairs = {}
 
-        def round_chunk(s, c):
+        def round_chunk(s, c, copy):
             g, t = divmod(s, PACK)
             if t == 0:
-                pairs[g, c] = placed([P, PACK * BANK], BF16, "pairs%d_%d" % (g, c), RAW_SECOND + c * 4 * KIB)
+                moved = g == 1 and c == CHUNKS - 1
+                offset = H_RING + 8 * KIB if moved else RAW_SECOND + c * 4 * KIB
+                pairs[g, c] = placed([P, PACK * BANK], BF16, "pairs%d_%d" % (g, c), offset)
             halves = pairs[g, c][:].rearrange("p (u m e) -> p u m e", u=2, e=2)
-            nc.scalar.copy(out=halves[:, t // 2, :, t % 2], in_=pages[s][:, c * BANK : (c + 1) * BANK])
+            values = pages[s][:, c * BANK : (c + 1) * BANK]
+            if t % 2 == 0:
+                twice = values.rearrange("p (m e) -> p m e", e=1).to_broadcast([P, BANK, 2])
+                copy(out=halves[:, t // 2, :, :], in_=twice)
+            else:
+                copy(out=halves[:, t // 2, :, 1], in_=values)
 
         def round_page(s):
             for c in range(CHUNKS):
-                round_chunk(s, c)
+                round_chunk(s, c, nc.scalar.copy)
 
         woven = {}
 
@@ -255,9 +271,11 @@ def tile_list_clause_prefix_cache_kernel(
             )
 
         page_codes = [kept([P, T2], U32, "page_codes%d" % g) for g in range(2)]
-        page_planes = [kept([P, T2], U8, "page_planes%d" % g) for g in range(2)]
+        page_planes = {}
 
         def quantize_chunk(g, c):
+            if c == 0:
+                page_planes[g] = placed([P, T2], U8, "page_planes%d" % g, SIXTH_HIDDEN + g * 2 * KIB)
             cols = slice(c * BANK, (c + 1) * BANK)
             nc.vector.quantize_mx(
                 out=page_codes[g][:, cols].bitcast(FP8X4), scales=page_planes[g][:, cols], in_=woven[g, c][:]
@@ -290,9 +308,23 @@ def tile_list_clause_prefix_cache_kernel(
                 stop=(g == 1),
             )
 
-        for s in range(PACK):
-            make_hidden(s)
-        scatter(0, 2)
+        first_hidden = [placed([P, BANK], F32, "first_hidden%d" % b, (H_RING, SIXTH_HIDDEN)[b]) for b in range(2)]
+        for b in range(2):
+            hidden_half(0, b, first_hidden[b][:])
+        turn_wgs(1)
+        repeat_and_turn_back(0, 1)
+        repeat_and_turn_back(1, 1)
+        keep_factor(0, 1)
+        make_hidden(1)
+        keep_factor(1, 1)
+        repeat_and_turn_back(2, 1)
+        repeat_and_turn_back(3, 1)
+        keep_factor(2, 1)
+        make_hidden(2)
+        keep_factor(3, 1)
+        make_hidden(3)
+        for b in range(2):
+            scatter_part(0, first_hidden[b][:], b * BANK, BANK)
         second_grouped = placed([P, 2 * PACK * PASS], BF16, "second_grouped", H_RING)
         for a in range(2):
             part = second_grouped[:, a * PACK * PASS : (a + 1) * PACK * PASS]
@@ -300,31 +332,31 @@ def tile_list_clause_prefix_cache_kernel(
         store_page(0)
         load_features(1)
         round_page(0)
-        scatter(1, 1)
+        scatter(1)
         store_page(1)
         load_page(6)
         round_page(1)
         for a in range(2):
             quantize_w1(a, 1)
-        scatter(2, 1)
+        scatter(2)
         store_page(2)
         load_features(2)
         make_hidden(4)
         round_page(2)
         make_hidden(5)
-        scatter(3, 1)
+        scatter(3)
         store_page(3)
         load_page(7)
         load_features(3)
         round_page(3)
-        make_hidden(6)
-        scatter(4, 1)
+        scatter(4)
         store_page(4)
         for c in range(CHUNKS):
             weave(0, c, nc.scalar.copy)
+        make_hidden(6)
         make_hidden(7)
         round_page(4)
-        scatter(5, 1)
+        scatter(5)
         store_page(5)
         for c in range(CHUNKS):
             quantize_chunk(0, c)
@@ -334,13 +366,15 @@ def tile_list_clause_prefix_cache_kernel(
         for n in range(N // P):
             for c in range(2):
                 layer_pass(n, c, 0)
-        scatter(6, 1)
+        scatter(6)
         store_page(6)
         round_page(6)
-        scatter(7, 1)
+        scatter(7)
         store_page(7)
 
-        round_page(7)
+        round_chunk(7, 0, nc.vector.tensor_copy)
+        for c in range(1, CHUNKS):
+            round_chunk(7, c, nc.scalar.copy)
         weave(1, 0, nc.vector.tensor_copy)
         weave(1, 1, nc.vector.tensor_copy)
         quantize_chunk(1, 0)

from contextlib import ExitStack

import concourse.mybir as mybir
from concourse.masks import make_identity

K, H, N, T, S, T2 = 1024, 1024, 512, 4096, 1024, 2048
FLOPS = 2 * K * H * S + 2 * H * N * T2

F32 = mybir.dt.float32
BF16 = mybir.dt.bfloat16
I32 = mybir.dt.int32
U32 = mybir.dt.uint32
U16 = mybir.dt.uint16
U8 = mybir.dt.uint8
FP8X4 = mybir.dt.float8_e4m3fn_x4
FP4X4 = mybir.dt.float4_e2m1fn_x4
MULT = mybir.AluOpType.mult
ADD = mybir.AluOpType.add
SILU = mybir.ActivationFunctionType.Silu

P = 128
PACK = 4
PASS = P * PACK
BANK = 512
KIB = 1024
QUADS = 4
SLICES = H // P
CHUNKS = T2 // BANK
RING = 4
ALIGN = 256

RAW_FIRST = 0
RAW_SECOND = 16 * KIB
TABLE = 32 * KIB
H_RING = 64 * KIB
Q_RING = 80 * KIB
SCALES = 96 * KIB
SECOND_HIDDEN = 100 * KIB
SIXTH_HIDDEN = 104 * KIB


def tile_list_clause_prefix_cache_kernel(
    tc, tab_words, tab_scales, offs, offs2, w1, wgs, page0, w2_words, w2_scales, slotf, out_0, out_1, out_2, out_3
):
    nc = tc.nc
    with ExitStack() as ctx:
        lists = ctx.enter_context(tc.tile_pool(name="lists", bufs=1))
        keep = ctx.enter_context(tc.tile_pool(name="keep", bufs=1))
        shared = ctx.enter_context(tc.tile_pool(name="shared", bufs=1))
        psum = ctx.enter_context(tc.psum_pool(name="psum", bufs=1))

        def kept(shape, dtype, name):
            return keep.tile(shape, dtype, name=name, align_bytes=ALIGN)

        def placed(shape, dtype, name, offset):
            return shared.tile(shape, dtype, name=name, offset=offset, align_bytes=ALIGN)

        def bank(number, name):
            return psum.tile([P, BANK], F32, name=name, tag="bank%d" % number)

        def page_rows(dram, s):
            g, t = divmod(s, PACK)
            return dram[g * PASS : (g + 1) * PASS, :].rearrange("(p t) m -> t p m", t=PACK)[t]

        def w1_rows(a, g):
            return w1[a * PASS : (a + 1) * PASS, g * PASS : (g + 1) * PASS].rearrange("(p j) c -> p j c", j=PACK)

        picks = lists.tile([P, S // 16], U16, name="picks")
        slots = lists.tile([P, S // 16], U16, name="slots")

        table_scales = placed([P, T], U8, "table_scales", SCALES)
        w2_planes = kept([P, 2, N], U8, "w2_planes")
        nc.vector.memset(table_scales[:].bitcast(I32), 0)
        nc.vector.memset(w2_planes[:].rearrange("p a c -> p (a c)").bitcast(I32), 0)
        identity = kept([P, P], F32, "identity")
        make_identity(nc, identity[:])

        warm = kept([P, 1], F32, "warm")
        nc.scalar.activation(warm[:], identity[:, 0:1], SILU)

        wgs_rows = [placed([P, BANK], F32, "wgs_rows%d" % b, Q_RING + (12 + 2 * b) * KIB) for b in range(2)]
        nc.sync.dma_start(out=wgs_rows[0][:], in_=wgs[:, 0:BANK])
        raw_first = [placed([P, PACK, PASS], F32, "raw_first%d" % a, RAW_FIRST + a * 8 * KIB) for a in range(2)]
        for a in range(2):
            for j in range(0, PACK, 2):
                nc.sync.dma_start(out=raw_first[a][:, j : j + 2, :], in_=w1_rows(a, 0)[:, j : j + 2, :])
        table = [placed([P, T], U32, "table%d" % a, TABLE + a * 16 * KIB) for a in range(2)]
        nc.sync.dma_start(picks[:], offs)
        nc.sync.dma_start(slots[:], offs2)
        words = [tab_words[a].rearrange("p n t -> p (n t)").bitcast(I32) for a in range(2)]
        for a in range(2):
            cols = slice(a * T // 2, (a + 1) * T // 2)
            nc.sync.dma_start(out=table[0][:, cols].bitcast(I32), in_=words[0][:, cols])
            for q in range(QUADS):
                nc.sync.dma_start(
                    out=table_scales[32 * q + 4 * a : 32 * q + 4 * a + 4, :].bitcast(I32),
                    in_=tab_scales[a, 4 * q : 4 * q + 4, :].bitcast(I32),
                )
        nc.sync.dma_start(out=table[1][:].bitcast(I32), in_=words[1])
        nc.sync.dma_start(out=wgs_rows[1][:], in_=wgs[:, BANK:S])
        pages = [kept([P, T2], F32, "page%d" % s) for s in range(SLICES)]

        def load_page(s):
            nc.sync.dma_start(out=pages[s][:], in_=page_rows(page0, s))

        load_page(0)
        load_page(1)
        raw_second = placed([P, 2, PACK, PASS], F32, "raw_second", RAW_SECOND)
        for a in range(2):
            nc.sync.dma_start(out=raw_second[:, a, :, :], in_=w1_rows(a, 1))
        w2_codes = kept([P, 2, 2 * N], U8, "w2_codes")
        nc.sync.dma_start(out=w2_codes[:].bitcast(I32), in_=w2_words.rearrange("a p c -> p a c").bitcast(I32))
        for q in range(QUADS):
            nc.sync.dma_start(
                out=w2_planes[32 * q : 32 * q + 4, :, :].bitcast(I32),
                in_=w2_scales[:, 4 * q : 4 * q + 4, :].rearrange("a r c -> r a c").bitcast(I32),
            )

        factor_rows = [kept([P, S], F32, "factor%d" % t) for t in range(PACK)]
        turned = {}
        back = {}

        def turn_wgs(b):
            turned[b] = bank(6 + b, "turned%d" % b)
            for j in range(4):
                nc.tensor.transpose(turned[b][:, j * P : (j + 1) * P], wgs_rows[b][:, j * P : (j + 1) * P], identity[:])

        def repeat_and_turn_back(t, b):
            repeated = placed([P, BANK], F32, "repeated%d_%d" % (t, b), Q_RING + (8 + 2 * (t % 2)) * KIB)
            picked = turned[b][:].rearrange("p (j q t) -> p j t q", j=4, t=PACK)[:, :, t : t + 1, :]
            nc.scalar.copy(
                out=repeated[:].rearrange("p (j r q) -> p j r q", j=4, r=QUADS),
                in_=picked.to_broadcast([P, 4, QUADS, 32]),
            )
            back[t, b] = bank(2 + t, "back%d_%d" % (t, b))
            for j in range(4):
                nc.tensor.transpose(back[t, b][:, j * P : (j + 1) * P], repeated[:, j * P : (j + 1) * P], identity[:])

        def keep_factor(t, b):
            nc.scalar.copy(out=factor_rows[t][:, b * BANK : (b + 1) * BANK], in_=back[t, b][:])

        turn_wgs(0)
        for t in range(PACK):
            repeat_and_turn_back(t, 0)
            if t > 0:
                keep_factor(t - 1, 0)
        keep_factor(PACK - 1, 0)

        w1_codes = {}
        w1_planes = {}
        w1_grouped = {}

        def group_w1(a, g, raw, grouped, copy):
            copy(
                out=grouped.rearrange("p (t m j) -> p m j t", t=PACK, j=PACK),
                in_=raw.rearrange("p j (m t) -> p m j t", t=PACK),
            )
            w1_grouped[a, g] = grouped

        def quantize_w1(a, g):
            if g == 0:
                w1_codes[a, g] = kept([P, PASS], U32, "w1_codes%d_%d" % (a, g))
            else:
                w1_codes[a, g] = placed([P, PASS], U32, "w1_codes%d_%d" % (a, g), SECOND_HIDDEN + a * 2 * KIB)
            w1_planes[a, g] = kept([P, PASS], U8, "w1_planes%d_%d" % (a, g))
            nc.vector.quantize_mx(
                out=w1_codes[a, g][:].bitcast(FP8X4), scales=w1_planes[a, g][:], in_=w1_grouped[a, g]
            )

        for a in range(2):
            grouped = placed([P, PACK * PASS], BF16, "w1_grouped%d" % a, Q_RING + a * 4 * KIB)
            group_w1(a, 0, raw_first[a][:], grouped[:], nc.vector.tensor_copy)
        for a in range(2):
            quantize_w1(a, 0)

        features = {}

        def load_features(n):
            offset = RAW_FIRST + n * 8 * KIB if n < 2 else TABLE + n * 8 * KIB
            features[n] = placed([P, T2], F32, "features%d" % n, offset)
            nc.sync.dma_start(out=features[n][:], in_=slotf[n * P : (n + 1) * P, :])

        load_features(0)
        for s in range(2, 6):
            load_page(s)

        first_words = kept([P, S], U32, "first_words")
        nc.vector.tensor_copy(first_words[:], table[0][:].indirect(picks[:]))
        picked_scales = placed([P, S], U8, "picked_scales", TABLE)
        nc.vector.tensor_copy(picked_scales[:], table_scales[:].indirect(picks[:]))
        picked_words = {}
        for b in range(2):
            picked_words[0, b] = first_words[:, b * BANK : (b + 1) * BANK]
            second_words = placed([P, BANK], U32, "second_words%d" % b, SCALES + b * 2 * KIB)
            nc.vector.tensor_copy(second_words[:], table[1][:].indirect(picks[:, 32 * b : 32 * (b + 1)]))
            picked_words[1, b] = second_words[:]

        hidden = {}
        hidden_at = {
            1: SECOND_HIDDEN,
            2: H_RING + 8 * KIB,
            3: H_RING + 12 * KIB,
            4: H_RING + 4 * KIB,
            5: SIXTH_HIDDEN,
            6: RAW_SECOND + 12 * KIB,
            7: H_RING + 12 * KIB,
        }

        def hidden_half(s, b, target):
            g, t = divmod(s, PACK)
            rows = slice(t * P, (t + 1) * P)
            acc = bank(b, "h%d_%d" % (s, b))
            for a in range(2):
                nc.tensor.matmul_mx(
                    out=acc[:],
                    lhsT=w1_codes[a, g][:, rows].bitcast(FP8X4),
                    lhsT_scale=w1_planes[a, g][:, rows],
                    rhs=picked_words[a, b].bitcast(FP8X4),
                    rhs_scale=picked_scales[4 * a : P, b * BANK : (b + 1) * BANK],
                    start=(a == 0),
                    stop=(a == 1),
                )
            nc.scalar.copy(out=target, in_=acc[:])

        def make_hidden(s):
            hidden[s] = placed([P, S], F32, "hidden%d" % s, hidden_at[s])
            for b in range(2):
                hidden_half(s, b, hidden[s][:, b * BANK : (b + 1) * BANK])

        def scatter_part(s, values, first, width):
            nc.vector.tensor_tensor(
                pages[s][:].indirect(slots[:, first // 16 : (first + width) // 16]),
                values,
                factor_rows[s % PACK][:, first : first + width],
                MULT,
            )

        def scatter(s):
            scatter_part(s, hidden[s][:], 0, S)

        def store_page(s):
            nc.sync.dma_start(out=page_rows(out_1, s), in_=pages[s][:])

        pairs = {}

        def round_chunk(s, c, copy):
            g, t = divmod(s, PACK)
            if t == 0:
                moved = g == 1 and c == CHUNKS - 1
                offset = H_RING + 8 * KIB if moved else RAW_SECOND + c * 4 * KIB
                pairs[g, c] = placed([P, PACK * BANK], BF16, "pairs%d_%d" % (g, c), offset)
            halves = pairs[g, c][:].rearrange("p (u m e) -> p u m e", u=2, e=2)
            values = pages[s][:, c * BANK : (c + 1) * BANK]
            if t % 2 == 0:
                twice = values.rearrange("p (m e) -> p m e", e=1).to_broadcast([P, BANK, 2])
                copy(out=halves[:, t // 2, :, :], in_=twice)
            else:
                copy(out=halves[:, t // 2, :, 1], in_=values)

        def round_page(s):
            for c in range(CHUNKS):
                round_chunk(s, c, nc.scalar.copy)

        woven = {}

        def weave(g, c, copy):
            woven[g, c] = placed([P, PACK * BANK], BF16, "woven%d_%d" % (g, c), Q_RING + c * 4 * KIB)
            copy(
                out=woven[g, c][:].bitcast(F32).rearrange("p (m u) -> p m u", u=2),
                in_=pairs[g, c][:].bitcast(F32).rearrange("p (u m) -> p m u", u=2),
            )

        page_codes = [kept([P, T2], U32, "page_codes%d" % g) for g in range(2)]
        page_planes = {}

        def quantize_chunk(g, c):
            if c == 0:
                page_planes[g] = placed([P, T2], U8, "page_planes%d" % g, SIXTH_HIDDEN + g * 2 * KIB)
            cols = slice(c * BANK, (c + 1) * BANK)
            nc.vector.quantize_mx(
                out=page_codes[g][:, cols].bitcast(FP8X4), scales=page_planes[g][:, cols], in_=woven[g, c][:]
            )

        def store_codes(g, cols):
            words = out_2[g].rearrange("p m t -> p (m t)").bitcast(I32)
            nc.sync.dma_start(out=words[:, cols], in_=page_codes[g][:, cols].bitcast(I32))

        def store_planes(g):
            for q in range(QUADS):
                nc.sync.dma_start(
                    out=out_3[g, 4 * q : 4 * q + 4, :].bitcast(I32),
                    in_=page_planes[g][32 * q : 32 * q + 4, :].bitcast(I32),
                )

        sums = {}

        def layer_pass(n, c, g):
            if g == 0:
                sums[n, c] = bank(2 * n + c % 2, "z%d_%d" % (n, c))
            cols = slice(c * BANK, (c + 1) * BANK)
            nc.tensor.matmul_mx(
                out=sums[n, c][:],
                lhsT=w2_codes[:, g, 2 * n * P : 2 * (n + 1) * P].bitcast(FP4X4),
                lhsT_scale=w2_planes[:, g, n * P : (n + 1) * P],
                rhs=page_codes[g][:, cols].bitcast(FP8X4),
                rhs_scale=page_planes[g][:, cols],
                start=(g == 0),
                stop=(g == 1),
            )

        first_hidden = [placed([P, BANK], F32, "first_hidden%d" % b, (H_RING, SIXTH_HIDDEN)[b]) for b in range(2)]
        for b in range(2):
            hidden_half(0, b, first_hidden[b][:])
        turn_wgs(1)
        repeat_and_turn_back(0, 1)
        repeat_and_turn_back(1, 1)
        keep_factor(0, 1)
        make_hidden(1)
        keep_factor(1, 1)
        repeat_and_turn_back(2, 1)
        repeat_and_turn_back(3, 1)
        keep_factor(2, 1)
        make_hidden(2)
        keep_factor(3, 1)
        make_hidden(3)
        for b in range(2):
            scatter_part(0, first_hidden[b][:], b * BANK, BANK)
        second_grouped = placed([P, 2 * PACK * PASS], BF16, "second_grouped", H_RING)
        for a in range(2):
            part = second_grouped[:, a * PACK * PASS : (a + 1) * PACK * PASS]
            group_w1(a, 1, raw_second[:, a, :, :], part, nc.scalar.copy)
        store_page(0)
        load_features(1)
        round_page(0)
        scatter(1)
        store_page(1)
        load_page(6)
        round_page(1)
        for a in range(2):
            quantize_w1(a, 1)
        scatter(2)
        store_page(2)
        load_features(2)
        make_hidden(4)
        round_page(2)
        make_hidden(5)
        scatter(3)
        store_page(3)
        load_page(7)
        load_features(3)
        round_page(3)
        scatter(4)
        store_page(4)
        for c in range(CHUNKS):
            weave(0, c, nc.scalar.copy)
        make_hidden(6)
        make_hidden(7)
        round_page(4)
        scatter(5)
        store_page(5)
        for c in range(CHUNKS):
            quantize_chunk(0, c)
        store_codes(0, slice(0, T2))
        store_planes(0)
        round_page(5)
        for n in range(N // P):
            for c in range(2):
                layer_pass(n, c, 0)
        scatter(6)
        store_page(6)
        round_page(6)
        scatter(7)
        store_page(7)

        round_chunk(7, 0, nc.vector.tensor_copy)
        for c in range(1, CHUNKS):
            round_chunk(7, c, nc.scalar.copy)
        weave(1, 0, nc.vector.tensor_copy)
        weave(1, 1, nc.vector.tensor_copy)
        quantize_chunk(1, 0)
        weave(1, 2, nc.vector.tensor_copy)
        quantize_chunk(1, 1)
        store_codes(1, slice(0, T2 // 2))
        weave(1, 3, nc.scalar.copy)
        quantize_chunk(1, 2)
        quantize_chunk(1, 3)
        store_codes(1, slice(T2 // 2, T2))
        store_planes(1)
        for half in range(2):
            for n in range(N // P):
                activated = placed([P, 2 * BANK], F32, "activated%d_%d" % (half, n), H_RING + n * 4 * KIB)
                for b in range(2):
                    c = 2 * half + b
                    if half == 1:
                        layer_pass(n, c, 0)
                    layer_pass(n, c, 1)
                    nc.scalar.activation(activated[:, b * BANK : (b + 1) * BANK], sums[n, c][:], SILU)
                    cols = slice(c * BANK, (c + 1) * BANK)
                    nc.vector.tensor_tensor(
                        features[n][:, cols], activated[:, b * BANK : (b + 1) * BANK], features[n][:, cols], ADD
                    )
                    last = half == 1 and n == N // P - 1
                    if last or b == 1:
                        cols = cols if last else slice(half * 2 * BANK, (half + 1) * 2 * BANK)
                        nc.sync.dma_start(out=out_0[n * P : (n + 1) * P, cols], in_=features[n][:, cols])
